import numpy as np
import ml_dtypes


def mxq(x, axis, fmt="e4m3"):
    dtype, down = {"e4m3": (ml_dtypes.float8_e4m3fn, 7), "e5m2": (ml_dtypes.float8_e5m2, 14)}[fmt]
    v = np.moveaxis(np.asarray(x, np.float32).astype(ml_dtypes.bfloat16).astype(np.float64), axis, -1)
    blocks = v.reshape(v.shape[:-1] + (-1, 32))
    amax = np.abs(blocks).max(-1, keepdims=True)
    byte = np.maximum(np.where(amax > 0, np.frexp(amax)[1] - 1 + 127, 0) - down, 1)
    scale = np.exp2(byte - 127.0)
    codes = (blocks / scale).astype(np.float32).astype(dtype).astype(np.float64)
    return np.moveaxis((codes * scale).reshape(v.shape), -1, axis)


WIDE = False


def mx_kscale(k):
    if not WIDE:
        return np.ones(k)
    levels = np.array([10, -10, 5, -5, 0])
    if k % 512:
        return np.exp2(np.random.permutation(np.resize(levels, k // 32))).repeat(32)
    a = np.empty((k // 512, 16))
    for p in range(k // 512):
        a[p, :8] = np.random.permutation(np.resize(levels, 8))
        for g in range(8):
            far = levels[np.abs(levels - a[p, g]) >= 10]
            a[p, g + 8] = far[np.random.randint(len(far))]
    return np.exp2(a.ravel()).repeat(32)


def f64(x):
    return np.asarray(x).astype(np.float64)


def striped(idx):
    return np.tile(np.asarray(idx).reshape(-1, 16).T, (8, 1)).astype(np.uint16)


def unstriped(offs):
    return offs[:16].T.reshape(-1).astype(np.int64)


E2M1 = np.array([0.0, 0.5, 1.0, 1.5, 2.0, 3.0, 4.0, 6.0, -0.0, -0.5, -1.0, -1.5, -2.0, -3.0, -4.0, -6.0])


def pack_weight(w, fmt):
    k, n = w.shape
    w = f64(np.asarray(w, np.float32).astype(ml_dtypes.bfloat16)).reshape(k // 32, 32, n)
    amax = np.abs(w).max(1)
    if fmt == "e4m3":
        byte = np.frexp(amax)[1] - 1 + 127 - 7
    else:
        mant, ex = np.frexp(amax / 6.0)
        byte = np.where(mant > 0.5, ex, ex - 1) + 127
    byte = np.clip(np.where(amax > 0, byte, 1), 1, 254)
    scaled = (w * np.exp2(127.0 - byte)[:, None, :]).reshape(k, n).astype(np.float32)
    by_word = np.ascontiguousarray(scaled.reshape(k // 512, 128, 4, n).transpose(0, 1, 3, 2))
    if fmt == "e4m3":
        words = by_word.astype(ml_dtypes.float8_e4m3fn).view(np.uint8)
    else:
        c = by_word.astype(ml_dtypes.float4_e2m1fn).view(np.uint8) & 0xF
        words = (c[..., 0::2] | (c[..., 1::2] << 4)).reshape(k // 512, 128, 2 * n)
    return np.ascontiguousarray(words), np.ascontiguousarray(byte.astype(np.uint8).reshape(k // 512, 16, n))


def unpack_weight(words, scales, fmt):
    g, _, n = scales.shape
    words = np.ascontiguousarray(words).reshape(g, 128, n, -1)
    if fmt == "e4m3":
        vals = words.view(ml_dtypes.float8_e4m3fn).astype(np.float64)
    else:
        nib = np.empty((g, 128, n, 4), np.uint8)
        nib[..., 0::2] = words & 0xF
        nib[..., 1::2] = words >> 4
        vals = E2M1[nib]
    vals = vals * np.repeat(np.exp2(scales.astype(np.float64) - 127.0), 8, axis=1)[..., None]
    return vals.transpose(0, 1, 3, 2).reshape(g * 512, n)


def bf(x):
    return np.asarray(x, np.float32).astype(ml_dtypes.bfloat16)


def planes(Y):
    r, m = Y.shape
    b = f64(bf(Y)).reshape(r // 32, 32, m)
    amax = np.abs(b).max(1)
    byte = np.clip(np.where(amax > 0, np.frexp(amax)[1] - 1 + 127 - 7, 1), 1, 254)
    codes = (b * np.exp2(127.0 - byte)[:, None, :]).reshape(r, m).astype(np.float32).astype(ml_dtypes.float8_e4m3fn).view(np.uint8)
    words = codes.reshape(r // 512, 128, 4, m).transpose(0, 1, 3, 2)
    return np.ascontiguousarray(words), np.ascontiguousarray(byte.astype(np.uint8).reshape(r // 512, 16, m))


K, T, J, B, N = 512, 2048, 2048, 512, 512


def setup_inputs():
    n = np.random.standard_normal
    idx = np.random.randint(0, T, J)
    fk = mx_kscale(K)
    wap = pack_weight(n((K, N)) * 1 / np.sqrt(K) / fk[:, None], "e4m3")
    wbp = pack_weight(n((K, N)) * 1 / np.sqrt(K) / fk[:, None], "e2m1")
    return {
        "xt": (n((K, T))).astype(np.float32),
        "fa": (np.random.uniform(0.5, 2.0, (K, 1)) * fk[:, None]).astype(np.float32),
        "fb": (np.random.uniform(0.5, 2.0, (K, 1)) * fk[:, None]).astype(np.float32),
        "wa_words": wap[0],
        "wa_scales": wap[1],
        "wb_words": wbp[0],
        "wb_scales": wbp[1],
        "offs": striped(idx),
    }


def reference(xt, fa, fb, wa_words, wa_scales, wb_words, wb_scales, offs):
    idx = unstriped(offs)
    wau = unpack_weight(wa_words, wa_scales, "e4m3")
    wbu = unpack_weight(wb_words, wb_scales, "e2m1")
    m = f64(xt)[:, idx].reshape(K, B, J // B).mean(axis=2)
    mr = np.repeat(m, J // B, axis=1)
    d = np.square(f64(xt)[:, idx] - mr)
    u = d.reshape(K, B, J // B).mean(axis=2) * f64(fa)
    v = m * f64(fb)
    uq = mxq(u, 0, "e4m3")
    vq = mxq(v, 0, "e4m3")
    y = wau.T @ uq + wbu.T @ vq
    words, scales = planes(y)
    return y, words, scales

@@ -1,0 +1,191 @@
+from contextlib import ExitStack
+
+import concourse.mybir as mybir
+from concourse.masks import make_identity
+
+K, T, J, B, N = 512, 2048, 2048, 512, 512
+FLOPS = 2 * 2 * K * N * B
+
+F32 = mybir.dt.float32
+BF16 = mybir.dt.bfloat16
+I32 = mybir.dt.int32
+U32 = mybir.dt.uint32
+U16 = mybir.dt.uint16
+U8 = mybir.dt.uint8
+E4M3 = mybir.dt.float8_e4m3fn_x4
+E2M1 = mybir.dt.float4_e2m1fn_x4
+ACT = mybir.ActivationFunctionType
+ALU = mybir.AluOpType
+
+P = 128
+PACK = 4
+GROUP = J // B
+CHUNK = 128
+CHUNKS = B // CHUNK
+WA_ROW = 4
+
+ITEMS = [(0, 0, 128, "h"), (0, 128, 128, "h"), (0, 256, 256, "h")] + [(t, b0, 256, "h") for t in (1, 2) for b0 in (0, 256)] + [(3, 0, 128, "h"), (3, 128, 128, "h"), (3, 256, 128, "h"), (3, 384, 128, "v")]
+
+
+def tile_list_group_spread_pl_kernel(tc, xt, fa, fb, wa_words, wa_scales, wb_words, wb_scales, offs, out_0, out_1, out_2):
+    nc = tc.nc
+    with ExitStack() as ctx:
+        keep = ctx.enter_context(tc.tile_pool(name="keep", bufs=1))
+        ring = ctx.enter_context(tc.tile_pool(name="ring", bufs=2))
+        psum = ctx.enter_context(tc.psum_pool(name="psum", bufs=1))
+
+        offsets = keep.tile([P, J // 16], U16, name="offsets")
+        nc.sync.dma_start(offsets[:], offs)
+        x_rows = xt.rearrange("(p t) c -> p t c", t=PACK)
+        planes = [keep.tile([P, T], F32, name=f"plane{t}") for t in range(PACK)]
+        nc.sync.dma_start(out=planes[0][:], in_=x_rows[:, 0, :])
+
+        wa_raw = keep.tile([P, N], I32, name="wa_raw")
+        wb_raw = keep.tile([P, 2 * N], U8, name="wb_raw")
+        ws_raw = keep.tile([P, N], U8, name="ws_raw")
+        fa_sb = keep.tile([P, PACK], F32, name="fa_sb")
+        fb_sb = keep.tile([P, PACK], F32, name="fb_sb")
+        nc.vector.memset(ws_raw[:].bitcast(I32), 0)
+        nc.scalar.dma_start(out=fa_sb[:], in_=fa.rearrange("(p t) o -> p (t o)", t=PACK))
+        nc.scalar.dma_start(out=fb_sb[:], in_=fb.rearrange("(p t) o -> p (t o)", t=PACK))
+        nc.sync.dma_start(out=planes[1][:], in_=x_rows[:, 1, :])
+        nc.sync.dma_start(out=planes[2][:], in_=x_rows[:, 2, :])
+        nc.sync.dma_start(out=planes[3][:], in_=x_rows[:, 3, :])
+        nc.sync.dma_start(out=wa_raw[:], in_=wa_words[0].rearrange("p n r -> p (n r)").bitcast(I32))
+        nc.sync.dma_start(out=wb_raw[:].bitcast(I32), in_=wb_words[0].bitcast(I32))
+        for q in range(4):
+            nc.sync.dma_start(out=ws_raw[32 * q : 32 * q + 4, :].bitcast(I32), in_=wb_scales[0, 4 * q : 4 * q + 4, :].bitcast(I32))
+            nc.sync.dma_start(out=ws_raw[32 * q + WA_ROW : 32 * q + WA_ROW + 4, :].bitcast(I32), in_=wa_scales[0, 4 * q : 4 * q + 4, :].bitcast(I32))
+
+        ident = keep.tile([P, P], F32, name="ident")
+        make_identity(nc, ident[:])
+        fa8 = keep.tile([P, PACK], F32, name="fa8")
+        fb4 = keep.tile([P, PACK], F32, name="fb4")
+        nc.scalar.mul(fa8[:], fa_sb[:], 0.125)
+        nc.scalar.mul(fb4[:], fb_sb[:], 0.25)
+
+        spread = [psum.tile([P, PACK, CHUNK], F32, name=f"spread{c}", tag=f"bank{c}") for c in range(CHUNKS)]
+        v_planes = keep.tile([P, PACK, B], BF16, name="v_planes")
+
+        def add_transposed(out, terms):
+            for i, term in enumerate(terms):
+                nc.tensor.matmul(out, lhsT=term, rhs=ident[:], is_transpose=True, start=(i == 0), stop=(i == len(terms) - 1))
+
+        state = {}
+
+        def gather(n):
+            t, b0, nb, eng = ITEMS[n]
+            g = ring.tile([P, GROUP, nb], F32, name="g", tag="g", bufs=3)
+            cols = slice(b0 * GROUP // 16, (b0 + nb) * GROUP // 16)
+            nc.vector.tensor_copy(g[:].bitcast(U32).rearrange("p i b -> p b i"), planes[t][:].bitcast(U32).indirect(offsets[:, cols]))
+            state[n] = g
+
+        def differences(n):
+            t, b0, nb, eng = ITEMS[n]
+            on_vector = eng == "v"
+            engine = nc.vector if on_vector else nc.gpsimd
+            pairs = state[n][:].rearrange("p (h e) b -> p h e b", e=2)
+            neg = ring.tile([P, 2, nb], F32, name="neg", tag="neg", bufs=1)
+            nc.scalar.mul(neg[:], pairs[:, :, 1, :], -1.0)
+            halves = ring.tile([P, 2, nb], F32, name="halves", tag="halves" + eng, bufs=2)
+            engine.tensor_tensor(halves[:], pairs[:, :, 0, :], pairs[:, :, 1, :], ALU.add)
+            d3 = ring.tile([P, nb], F32, name="d3", tag="d3" + eng, bufs=2)
+            if eng == "h":
+                nc.scalar.mul(d3[:], halves[:, 1, :], -1.0)
+            else:
+                engine.tensor_tensor(d3[:], halves[:, 0, :], halves[:, 1, :], ALU.subtract)
+            total = ring.tile([P, nb], F32, name="total", tag="total" + eng, bufs=2)
+            engine.tensor_tensor(total[:], halves[:, 0, :], halves[:, 1, :], ALU.add)
+            da = psum.tile([P, nb // CHUNK, 2, P], F32, name="da", tag="da", bufs=2)
+            db = psum.tile([P, nb // CHUNK, P], F32, name="db", tag="db", bufs=2)
+            for k in range(nb // CHUNK):
+                blk = slice(k * CHUNK, (k + 1) * CHUNK)
+                for h in range(2):
+                    add_transposed(da[:, k, h, :], [pairs[:, h, 0, blk], neg[:, h, blk]])
+            for k in range(nb // CHUNK):
+                blk = slice(k * CHUNK, (k + 1) * CHUNK)
+                add_transposed(db[:, k, :], [halves[:, 0, blk], d3[:, blk]] if eng == "h" else [d3[:, blk]])
+            state[n] = (da, db, total)
+
+        def squares(n):
+            t, b0, nb, eng = ITEMS[n]
+            da, db, total = state[n]
+            qa = ring.tile([P, nb // CHUNK, 2, P], F32, name="qa", tag="qa", bufs=2)
+            qb = ring.tile([P, nb // CHUNK, P], F32, name="qb", tag="qb", bufs=2)
+            nc.scalar.activation(qa[:], da[:], ACT.Square)
+            nc.scalar.activation(qb[:], db[:], ACT.Square, scale=0.5**0.5)
+            nc.scalar.activation(v_planes[:, t, b0 : b0 + nb], total[:], ACT.Copy, scale=fb4[:, t : t + 1])
+            for k in range(nb // CHUNK):
+                add_transposed(spread[b0 // CHUNK + k][:, t, :], [qa[:, k, 0, :], qa[:, k, 1, :], qb[:, k, :]])
+
+        wa = keep.tile([P, PACK, P], I32, name="wa", align_bytes=64)
+        wb = keep.tile([P, PACK, P, 2], U8, name="wb", align_bytes=64)
+        ws = keep.tile([P, PACK, P], U8, name="ws", align_bytes=64)
+
+        def deal_weights():
+            nc.vector.tensor_copy(wa[:], wa_raw[:].rearrange("p (m t) -> p t m", t=PACK))
+            nc.vector.tensor_copy(wb[:], wb_raw[:].rearrange("p (m t e) -> p t m e", t=PACK, e=2))
+            nc.vector.tensor_copy(ws[:], ws_raw[:].rearrange("p (m t) -> p t m", t=PACK))
+
+        y_codes = keep.tile([P, B], U32, name="y_codes", align_bytes=64)
+        y_scales = keep.tile([P, B], U8, name="y_scales", align_bytes=64)
+        out_rows = out_0.rearrange("(p t) b -> p t b", t=PACK)
+        out_words = out_1[0].rearrange("p b r -> p (b r)").bitcast(I32)
+
+        def quantise(src, name):
+            codes = ring.tile([P, CHUNK], U32, name=name + "_codes", tag=name + "_codes", bufs=CHUNKS, align_bytes=64)
+            scales = ring.tile([P, CHUNK], U8, name=name + "_scales", tag=name + "_scales", bufs=CHUNKS, align_bytes=64)
+            nc.vector.quantize_mx(out=codes[:].bitcast(E4M3), scales=scales[:], in_=src[:].rearrange("p b t -> p (b t)"))
+            return codes, scales
+
+        def operands(c):
+            cols = slice(c * CHUNK, (c + 1) * CHUNK)
+            v = ring.tile([P, CHUNK, PACK], BF16, name="v", tag="v", bufs=CHUNKS, align_bytes=64)
+            nc.vector.tensor_copy(
+                v[:].rearrange("p (c i) t -> p c t i", i=4), v_planes[:, :, cols].rearrange("p t (c i) -> p c t i", i=4)
+            )
+            u = ring.tile([P, CHUNK, PACK], BF16, name="u", tag="u", bufs=CHUNKS, align_bytes=64)
+            nc.vector.tensor_tensor(
+                u[:], spread[c][:].rearrange("p t b -> p b t"), fa8[:].unsqueeze(1).to_broadcast([P, CHUNK, PACK]), ALU.mult
+            )
+            state["q", c] = (quantise(v, "v"), quantise(u, "u"))
+
+        def product(c):
+            cols = slice(c * CHUNK, (c + 1) * CHUNK)
+            (v_codes, v_scales), (u_codes, u_scales) = state["q", c]
+            y = psum.tile([P, PACK, CHUNK], F32, name="y", tag=f"bank{c}", bufs=1)
+            for t in range(PACK):
+                nc.tensor.matmul_mx(
+                    out=y[:, t, :], lhsT=wb[:, t, :, :].rearrange("p m e -> p (m e)").bitcast(E2M1), lhsT_scale=ws[:, t, :],
+                    rhs=v_codes[:].bitcast(E4M3), rhs_scale=v_scales[:], start=(t == 0), stop=False,
+                )
+            for t in range(PACK):
+                nc.tensor.matmul_mx(
+                    out=y[:, t, :], lhsT=wa[:, t, :].bitcast(E4M3), lhsT_scale=ws[WA_ROW:P, t, :],
+                    rhs=u_codes[:].bitcast(E4M3), rhs_scale=u_scales[:], start=False, stop=(t == PACK - 1),
+                )
+            y16 = ring.tile([P, CHUNK, PACK], BF16, name="y16", tag="y16", bufs=CHUNKS, align_bytes=64)
+            nc.scalar.copy(y16[:], y[:].rearrange("p t b -> p b t"))
+            y32 = ring.tile([P, PACK, CHUNK], F32, name="y32", tag="y32", bufs=CHUNKS)
+            nc.scalar.copy(y32[:], y[:])
+            nc.sync.dma_start(out=out_rows[:, :, cols], in_=y32[:])
+            nc.vector.quantize_mx(
+                out=y_codes[:, cols].bitcast(E4M3), scales=y_scales[:, cols], in_=y16[:].rearrange("p b t -> p (b t)")
+            )
+            nc.sync.dma_start(out=out_words[:, cols], in_=y_codes[:, cols].bitcast(I32))
+
+        last = len(ITEMS)
+        for n in range(last + 1):
+            if n < last:
+                gather(n)
+                differences(n)
+            if n >= 1:
+                squares(n - 1)
+        deal_weights()
+        for c in range(CHUNKS):
+            operands(c)
+        for c in range(CHUNKS):
+            product(c)
+        for q in range(4):
+            queue = nc.sync if q % 2 == 0 else nc.scalar
+            queue.dma_start(out=out_2[0, 4 * q : 4 * q + 4, :].bitcast(I32), in_=y_scales[32 * q : 32 * q + 4, :].bitcast(I32))

@@ -24,7 +24,7 @@ CHUNK = 128
 CHUNKS = B // CHUNK
 WA_ROW = 4
 
-ITEMS = [(0, 0, 128, "h"), (0, 128, 128, "h"), (0, 256, 256, "h")] + [(t, b0, 256, "h") for t in (1, 2) for b0 in (0, 256)] + [(3, 0, 128, "h"), (3, 128, 128, "h"), (3, 256, 128, "h"), (3, 384, 128, "v")]
+ITEMS = [(t, b0, 256, "h" if t == 0 else "g") for t in range(3) for b0 in (0, 256)]
 
 
 def tile_list_group_spread_pl_kernel(tc, xt, fa, fb, wa_words, wa_scales, wb_words, wb_scales, offs, out_0, out_1, out_2):
@@ -38,24 +38,36 @@ def tile_list_group_spread_pl_kernel(tc, xt, fa, fb, wa_words, wa_scales, wb_wor
         nc.sync.dma_start(offsets[:], offs)
         x_rows = xt.rearrange("(p t) c -> p t c", t=PACK)
         planes = [keep.tile([P, T], F32, name=f"plane{t}") for t in range(PACK)]
-        nc.sync.dma_start(out=planes[0][:], in_=x_rows[:, 0, :])
-
         wa_raw = keep.tile([P, N], I32, name="wa_raw")
         wb_raw = keep.tile([P, 2 * N], U8, name="wb_raw")
         ws_raw = keep.tile([P, N], U8, name="ws_raw")
         fa_sb = keep.tile([P, PACK], F32, name="fa_sb")
         fb_sb = keep.tile([P, PACK], F32, name="fb_sb")
         nc.vector.memset(ws_raw[:].bitcast(I32), 0)
-        nc.scalar.dma_start(out=fa_sb[:], in_=fa.rearrange("(p t) o -> p (t o)", t=PACK))
-        nc.scalar.dma_start(out=fb_sb[:], in_=fb.rearrange("(p t) o -> p (t o)", t=PACK))
-        nc.sync.dma_start(out=planes[1][:], in_=x_rows[:, 1, :])
-        nc.sync.dma_start(out=planes[2][:], in_=x_rows[:, 2, :])
-        nc.sync.dma_start(out=planes[3][:], in_=x_rows[:, 3, :])
-        nc.sync.dma_start(out=wa_raw[:], in_=wa_words[0].rearrange("p n r -> p (n r)").bitcast(I32))
-        nc.sync.dma_start(out=wb_raw[:].bitcast(I32), in_=wb_words[0].bitcast(I32))
-        for q in range(4):
-            nc.sync.dma_start(out=ws_raw[32 * q : 32 * q + 4, :].bitcast(I32), in_=wb_scales[0, 4 * q : 4 * q + 4, :].bitcast(I32))
-            nc.sync.dma_start(out=ws_raw[32 * q + WA_ROW : 32 * q + WA_ROW + 4, :].bitcast(I32), in_=wa_scales[0, 4 * q : 4 * q + 4, :].bitcast(I32))
+
+        def load_plane(t):
+            nc.sync.dma_start(out=planes[t][:], in_=x_rows[:, t, :])
+
+        def load_words(queue):
+            queue.dma_start(out=wb_raw[:].bitcast(I32), in_=wb_words[0].bitcast(I32))
+            queue.dma_start(out=wa_raw[:], in_=wa_words[0].rearrange("p n r -> p (n r)").bitcast(I32))
+
+        def load_scales(queue):
+            for q in range(4):
+                queue.dma_start(out=ws_raw[32 * q : 32 * q + 4, :].bitcast(I32), in_=wb_scales[0, 4 * q : 4 * q + 4, :].bitcast(I32))
+                queue.dma_start(out=ws_raw[32 * q + WA_ROW : 32 * q + WA_ROW + 4, :].bitcast(I32), in_=wa_scales[0, 4 * q : 4 * q + 4, :].bitcast(I32))
+
+        def load_factors(queue):
+            queue.dma_start(out=fb_sb[:], in_=fb.rearrange("(p t) o -> p (t o)", t=PACK))
+            queue.dma_start(out=fa_sb[:], in_=fa.rearrange("(p t) o -> p (t o)", t=PACK))
+
+        load_plane(0)
+        load_factors(nc.scalar)
+        load_plane(1)
+        load_plane(2)
+        load_plane(3)
+        load_words(nc.sync)
+        load_scales(nc.sync)
 
         ident = keep.tile([P, P], F32, name="ident")
         make_identity(nc, ident[:])
@@ -64,8 +76,7 @@ def tile_list_group_spread_pl_kernel(tc, xt, fa, fb, wa_words, wa_scales, wb_wor
         nc.scalar.mul(fa8[:], fa_sb[:], 0.125)
         nc.scalar.mul(fb4[:], fb_sb[:], 0.25)
 
-        spread = [psum.tile([P, PACK, CHUNK], F32, name=f"spread{c}", tag=f"bank{c}") for c in range(CHUNKS)]
-        v_planes = keep.tile([P, PACK, B], BF16, name="v_planes")
+        vu_planes = keep.tile([P, 2, PACK, B], BF16, name="vu_planes")
 
         def add_transposed(out, terms):
             for i, term in enumerate(terms):
@@ -73,38 +84,40 @@ def tile_list_group_spread_pl_kernel(tc, xt, fa, fb, wa_words, wa_scales, wb_wor
 
         state = {}
 
-        def gather(n):
-            t, b0, nb, eng = ITEMS[n]
-            g = ring.tile([P, GROUP, nb], F32, name="g", tag="g", bufs=3)
+        def gather(t, b0, nb):
+            g = keep.tile([P, nb, 2, 2], F32, name=f"g{t}_{b0}")
             cols = slice(b0 * GROUP // 16, (b0 + nb) * GROUP // 16)
-            nc.vector.tensor_copy(g[:].bitcast(U32).rearrange("p i b -> p b i"), planes[t][:].bitcast(U32).indirect(offsets[:, cols]))
-            state[n] = g
+            nc.vector.tensor_copy(g[:].rearrange("p b h e -> p (b h e)"), planes[t][:].indirect(offsets[:, cols]))
+            return g
 
         def differences(n):
             t, b0, nb, eng = ITEMS[n]
-            on_vector = eng == "v"
-            engine = nc.vector if on_vector else nc.gpsimd
-            pairs = state[n][:].rearrange("p (h e) b -> p h e b", e=2)
-            neg = ring.tile([P, 2, nb], F32, name="neg", tag="neg", bufs=1)
-            nc.scalar.mul(neg[:], pairs[:, :, 1, :], -1.0)
-            halves = ring.tile([P, 2, nb], F32, name="halves", tag="halves" + eng, bufs=2)
-            engine.tensor_tensor(halves[:], pairs[:, :, 0, :], pairs[:, :, 1, :], ALU.add)
-            d3 = ring.tile([P, nb], F32, name="d3", tag="d3" + eng, bufs=2)
-            if eng == "h":
-                nc.scalar.mul(d3[:], halves[:, 1, :], -1.0)
-            else:
-                engine.tensor_tensor(d3[:], halves[:, 0, :], halves[:, 1, :], ALU.subtract)
-            total = ring.tile([P, nb], F32, name="total", tag="total" + eng, bufs=2)
-            engine.tensor_tensor(total[:], halves[:, 0, :], halves[:, 1, :], ALU.add)
+            g = gather(t, b0, nb)
+            neg = ring.tile([P, 2, nb], F32, name="neg", tag="neg", bufs=2)
+            nc.scalar.mul(neg[:].rearrange("p h b -> p b h"), g[:, :, :, 1], -1.0)
+            halves = ring.tile([P, nb, 2], F32, name="halves", tag="halves", bufs=3)
+            nc.gpsimd.tensor_tensor(halves[:], g[:, :, :, 0], g[:, :, :, 1], ALU.add)
+            d3 = ring.tile([P, nb], F32, name="d3", tag="d3", bufs=3)
+            if eng != "h":
+                nc.gpsimd.tensor_tensor(d3[:], halves[:, :, 0], halves[:, :, 1], ALU.subtract)
+            total = ring.tile([P, nb], F32, name="total", tag="total", bufs=3)
+            nc.gpsimd.tensor_tensor(total[:], halves[:, :, 0], halves[:, :, 1], ALU.add)
             da = psum.tile([P, nb // CHUNK, 2, P], F32, name="da", tag="da", bufs=2)
-            db = psum.tile([P, nb // CHUNK, P], F32, name="db", tag="db", bufs=2)
             for k in range(nb // CHUNK):
                 blk = slice(k * CHUNK, (k + 1) * CHUNK)
                 for h in range(2):
-                    add_transposed(da[:, k, h, :], [pairs[:, h, 0, blk], neg[:, h, blk]])
+                    add_transposed(da[:, k, h, :], [g[:, blk, h, 0], neg[:, h, blk]])
+            state[n] = (da, halves, d3, total)
+
+        def third(n):
+            t, b0, nb, eng = ITEMS[n]
+            da, halves, d3, total = state[n]
+            if eng == "h":
+                nc.scalar.mul(d3[:], halves[:, :, 1], -1.0)
+            db = psum.tile([P, nb // CHUNK, P], F32, name="db", tag="db", bufs=2)
             for k in range(nb // CHUNK):
                 blk = slice(k * CHUNK, (k + 1) * CHUNK)
-                add_transposed(db[:, k, :], [halves[:, 0, blk], d3[:, blk]] if eng == "h" else [d3[:, blk]])
+                add_transposed(db[:, k, :], [halves[:, blk, 0], d3[:, blk]] if eng == "h" else [d3[:, blk]])
             state[n] = (da, db, total)
 
         def squares(n):
@@ -114,17 +127,44 @@ def tile_list_group_spread_pl_kernel(tc, xt, fa, fb, wa_words, wa_scales, wb_wor
             qb = ring.tile([P, nb // CHUNK, P], F32, name="qb", tag="qb", bufs=2)
             nc.scalar.activation(qa[:], da[:], ACT.Square)
             nc.scalar.activation(qb[:], db[:], ACT.Square, scale=0.5**0.5)
-            nc.scalar.activation(v_planes[:, t, b0 : b0 + nb], total[:], ACT.Copy, scale=fb4[:, t : t + 1])
+            nc.scalar.activation(vu_planes[:, 0, t, b0 : b0 + nb], total[:], ACT.Copy, scale=fb4[:, t : t + 1])
+            spread = psum.tile([P, nb], F32, name="spread", tag="spread", bufs=2)
             for k in range(nb // CHUNK):
-                add_transposed(spread[b0 // CHUNK + k][:, t, :], [qa[:, k, 0, :], qa[:, k, 1, :], qb[:, k, :]])
+                add_transposed(spread[:, k * CHUNK : (k + 1) * CHUNK], [qa[:, k, 0, :], qa[:, k, 1, :], qb[:, k, :]])
+            state[n] = spread
+
+        def spread_out(n):
+            t, b0, nb, eng = ITEMS[n]
+            nc.scalar.activation(vu_planes[:, 1, t, b0 : b0 + nb], state[n][:], ACT.Copy, scale=fa8[:, t : t + 1])
+
+        def last_plane(g, b0, nb):
+            t = PACK - 1
+            d12 = ring.tile([P, nb, 2], F32, name="d12", tag="d12")
+            nc.vector.tensor_tensor(d12[:], g[:, :, :, 0], g[:, :, :, 1], ALU.subtract)
+            s12 = ring.tile([P, nb, 2], F32, name="s12", tag="s12")
+            nc.vector.tensor_tensor(s12[:], g[:, :, :, 0], g[:, :, :, 1], ALU.add)
+            q12 = ring.tile([P, nb, 2], F32, name="q12", tag="q12")
+            nc.scalar.activation(q12[:], d12[:], ACT.Square)
+            e3 = ring.tile([P, nb], F32, name="e3", tag="e3")
+            nc.vector.tensor_tensor(e3[:], s12[:, :, 0], s12[:, :, 1], ALU.subtract)
+            s4 = ring.tile([P, nb], F32, name="s4", tag="s4")
+            nc.vector.tensor_tensor(s4[:], s12[:, :, 0], s12[:, :, 1], ALU.add)
+            q3 = ring.tile([P, nb], F32, name="q3", tag="q3")
+            nc.scalar.activation(q3[:], e3[:], ACT.Square, scale=0.5**0.5)
+            q3f = ring.tile([P, nb], F32, name="q3f", tag="q3f")
+            nc.scalar.activation(q3f[:], q3[:], ACT.Copy, scale=fa8[:, t : t + 1])
+            nc.scalar.activation(vu_planes[:, 0, t, b0 : b0 + nb], s4[:], ACT.Copy, scale=fb4[:, t : t + 1])
+            q = ring.tile([P, nb], F32, name="q", tag="q")
+            nc.vector.tensor_tensor(q[:], q12[:, :, 0], q12[:, :, 1], ALU.add)
+            nc.vector.scalar_tensor_tensor(vu_planes[:, 1, t, b0 : b0 + nb], q[:], fa8[:, t : t + 1], q3f[:], ALU.mult, ALU.add)
 
         wa = keep.tile([P, PACK, P], I32, name="wa", align_bytes=64)
         wb = keep.tile([P, PACK, P, 2], U8, name="wb", align_bytes=64)
         ws = keep.tile([P, PACK, P], U8, name="ws", align_bytes=64)
 
         def deal_weights():
+            nc.vector.tensor_copy(wb[:].rearrange("p t m e -> p t (m e)").bitcast(U16), wb_raw[:].bitcast(U16).rearrange("p (m t) -> p t m", t=PACK))
             nc.vector.tensor_copy(wa[:], wa_raw[:].rearrange("p (m t) -> p t m", t=PACK))
-            nc.vector.tensor_copy(wb[:], wb_raw[:].rearrange("p (m t e) -> p t m e", t=PACK, e=2))
             nc.vector.tensor_copy(ws[:], ws_raw[:].rearrange("p (m t) -> p t m", t=PACK))
 
         y_codes = keep.tile([P, B], U32, name="y_codes", align_bytes=64)
@@ -132,41 +172,36 @@ def tile_list_group_spread_pl_kernel(tc, xt, fa, fb, wa_words, wa_scales, wb_wor
         out_rows = out_0.rearrange("(p t) b -> p t b", t=PACK)
         out_words = out_1[0].rearrange("p b r -> p (b r)").bitcast(I32)
 
-        def quantise(src, name):
-            codes = ring.tile([P, CHUNK], U32, name=name + "_codes", tag=name + "_codes", bufs=CHUNKS, align_bytes=64)
-            scales = ring.tile([P, CHUNK], U8, name=name + "_scales", tag=name + "_scales", bufs=CHUNKS, align_bytes=64)
-            nc.vector.quantize_mx(out=codes[:].bitcast(E4M3), scales=scales[:], in_=src[:].rearrange("p b t -> p (b t)"))
-            return codes, scales
-
         def operands(c):
             cols = slice(c * CHUNK, (c + 1) * CHUNK)
-            v = ring.tile([P, CHUNK, PACK], BF16, name="v", tag="v", bufs=CHUNKS, align_bytes=64)
-            nc.vector.tensor_copy(
-                v[:].rearrange("p (c i) t -> p c t i", i=4), v_planes[:, :, cols].rearrange("p t (c i) -> p c t i", i=4)
-            )
-            u = ring.tile([P, CHUNK, PACK], BF16, name="u", tag="u", bufs=CHUNKS, align_bytes=64)
-            nc.vector.tensor_tensor(
-                u[:], spread[c][:].rearrange("p t b -> p b t"), fa8[:].unsqueeze(1).to_broadcast([P, CHUNK, PACK]), ALU.mult
-            )
-            state["q", c] = (quantise(v, "v"), quantise(u, "u"))
+            vu = ring.tile([P, 2, CHUNK, PACK], BF16, name="vu", tag="vu", bufs=CHUNKS, align_bytes=64)
+            for i in range(2):
+                nc.vector.tensor_copy(
+                    vu[:, i].rearrange("p (c j) t -> p c t j", j=4), vu_planes[:, i, :, cols].rearrange("p t (c j) -> p c t j", j=4)
+                )
+            codes = ring.tile([P, 2, CHUNK], U32, name="codes", tag="codes", bufs=CHUNKS, align_bytes=64)
+            scales = ring.tile([P, 2, CHUNK], U8, name="scales", tag="scales", bufs=CHUNKS, align_bytes=64)
+            for i in range(2):
+                nc.vector.quantize_mx(out=codes[:, i, :].bitcast(E4M3), scales=scales[:, i, :], in_=vu[:, i].rearrange("p b t -> p (b t)"))
+            state["q", c] = (codes, scales)
 
         def product(c):
             cols = slice(c * CHUNK, (c + 1) * CHUNK)
-            (v_codes, v_scales), (u_codes, u_scales) = state["q", c]
-            y = psum.tile([P, PACK, CHUNK], F32, name="y", tag=f"bank{c}", bufs=1)
+            codes, scales = state["q", c]
+            y = psum.tile([P, PACK, CHUNK], F32, name="y", tag="y", bufs=2)
             for t in range(PACK):
                 nc.tensor.matmul_mx(
                     out=y[:, t, :], lhsT=wb[:, t, :, :].rearrange("p m e -> p (m e)").bitcast(E2M1), lhsT_scale=ws[:, t, :],
-                    rhs=v_codes[:].bitcast(E4M3), rhs_scale=v_scales[:], start=(t == 0), stop=False,
+                    rhs=codes[:, 0, :].bitcast(E4M3), rhs_scale=scales[:, 0, :], start=(t == 0), stop=False,
                 )
             for t in range(PACK):
                 nc.tensor.matmul_mx(
                     out=y[:, t, :], lhsT=wa[:, t, :].bitcast(E4M3), lhsT_scale=ws[WA_ROW:P, t, :],
-                    rhs=u_codes[:].bitcast(E4M3), rhs_scale=u_scales[:], start=False, stop=(t == PACK - 1),
+                    rhs=codes[:, 1, :].bitcast(E4M3), rhs_scale=scales[:, 1, :], start=False, stop=(t == PACK - 1),
                 )
             y16 = ring.tile([P, CHUNK, PACK], BF16, name="y16", tag="y16", bufs=CHUNKS, align_bytes=64)
-            nc.scalar.copy(y16[:], y[:].rearrange("p t b -> p b t"))
             y32 = ring.tile([P, PACK, CHUNK], F32, name="y32", tag="y32", bufs=CHUNKS)
+            nc.scalar.copy(y16[:], y[:].rearrange("p t b -> p b t"))
             nc.scalar.copy(y32[:], y[:])
             nc.sync.dma_start(out=out_rows[:, :, cols], in_=y32[:])
             nc.vector.quantize_mx(
@@ -175,17 +210,23 @@ def tile_list_group_spread_pl_kernel(tc, xt, fa, fb, wa_words, wa_scales, wb_wor
             nc.sync.dma_start(out=out_words[:, cols], in_=y_codes[:, cols].bitcast(I32))
 
         last = len(ITEMS)
-        for n in range(last + 1):
+        for n in range(last + 2):
             if n < last:
-                gather(n)
                 differences(n)
-            if n >= 1:
+            if 2 <= n:
+                spread_out(n - 2)
+            if 1 <= n <= last:
                 squares(n - 1)
+            if n < last:
+                third(n)
+        tail = [(gather(PACK - 1, b0, 256), b0) for b0 in range(0, B, 256)]
         deal_weights()
-        for c in range(CHUNKS):
-            operands(c)
-        for c in range(CHUNKS):
-            product(c)
+        for g, b0 in tail:
+            last_plane(g, b0, 256)
+            for c in range(b0 // CHUNK, (b0 + 256) // CHUNK):
+                operands(c)
+            for c in range(b0 // CHUNK, (b0 + 256) // CHUNK):
+                product(c)
         for q in range(4):
             queue = nc.sync if q % 2 == 0 else nc.scalar
             queue.dma_start(out=out_2[0, 4 * q : 4 * q + 4, :].bitcast(I32), in_=y_scales[32 * q : 32 * q + 4, :].bitcast(I32))

@@ -24,7 +24,7 @@ CHUNK = 128
 CHUNKS = B // CHUNK
 WA_ROW = 4
 
-ITEMS = [(t, b0, 256, "h" if t == 0 else "g") for t in range(3) for b0 in (0, 256)]
+ITEMS = [(t, b0, 256, "g" if t == 1 else "h") for t in range(3) for b0 in (0, 256)]
 
 
 def tile_list_group_spread_pl_kernel(tc, xt, fa, fb, wa_words, wa_scales, wb_words, wb_scales, offs, out_0, out_1, out_2):
@@ -35,7 +35,6 @@ def tile_list_group_spread_pl_kernel(tc, xt, fa, fb, wa_words, wa_scales, wb_wor
         psum = ctx.enter_context(tc.psum_pool(name="psum", bufs=1))
 
         offsets = keep.tile([P, J // 16], U16, name="offsets")
-        nc.sync.dma_start(offsets[:], offs)
         x_rows = xt.rearrange("(p t) c -> p t c", t=PACK)
         planes = [keep.tile([P, T], F32, name=f"plane{t}") for t in range(PACK)]
         wa_raw = keep.tile([P, N], I32, name="wa_raw")
@@ -62,11 +61,12 @@ def tile_list_group_spread_pl_kernel(tc, xt, fa, fb, wa_words, wa_scales, wb_wor
             queue.dma_start(out=fa_sb[:], in_=fa.rearrange("(p t) o -> p (t o)", t=PACK))
 
         load_plane(0)
+        nc.sync.dma_start(offsets[:], offs)
+        load_words(nc.sync)
         load_factors(nc.scalar)
         load_plane(1)
         load_plane(2)
         load_plane(3)
-        load_words(nc.sync)
         load_scales(nc.sync)
 
         ident = keep.tile([P, P], F32, name="ident")
@@ -163,9 +163,9 @@ def tile_list_group_spread_pl_kernel(tc, xt, fa, fb, wa_words, wa_scales, wb_wor
         ws = keep.tile([P, PACK, P], U8, name="ws", align_bytes=64)
 
         def deal_weights():
-            nc.vector.tensor_copy(wb[:].rearrange("p t m e -> p t (m e)").bitcast(U16), wb_raw[:].bitcast(U16).rearrange("p (m t) -> p t m", t=PACK))
-            nc.vector.tensor_copy(wa[:], wa_raw[:].rearrange("p (m t) -> p t m", t=PACK))
-            nc.vector.tensor_copy(ws[:], ws_raw[:].rearrange("p (m t) -> p t m", t=PACK))
+            nc.gpsimd.tensor_copy(wb[:], wb_raw[:].rearrange("p (m t e) -> p t m e", t=PACK, e=2))
+            nc.gpsimd.tensor_copy(wa[:], wa_raw[:].rearrange("p (m t) -> p t m", t=PACK))
+            nc.gpsimd.tensor_copy(ws[:], ws_raw[:].rearrange("p (m t) -> p t m", t=PACK))
 
         y_codes = keep.tile([P, B], U32, name="y_codes", align_bytes=64)
         y_scales = keep.tile([P, B], U8, name="y_scales", align_bytes=64)
@@ -209,6 +209,7 @@ def tile_list_group_spread_pl_kernel(tc, xt, fa, fb, wa_words, wa_scales, wb_wor
             )
             nc.sync.dma_start(out=out_words[:, cols], in_=y_codes[:, cols].bitcast(I32))
 
+        deal_weights()
         last = len(ITEMS)
         for n in range(last + 2):
             if n < last:
@@ -220,7 +221,6 @@ def tile_list_group_spread_pl_kernel(tc, xt, fa, fb, wa_words, wa_scales, wb_wor
             if n < last:
                 third(n)
         tail = [(gather(PACK - 1, b0, 256), b0) for b0 in range(0, B, 256)]
-        deal_weights()
         for g, b0 in tail:
             last_plane(g, b0, 256)
             for c in range(b0 // CHUNK, (b0 + 256) // CHUNK):

@@ -20,11 +20,15 @@ ALU = mybir.AluOpType
 P = 128
 PACK = 4
 GROUP = J // B
+STRIPE = 16
+HALF = B // 2
 CHUNK = 128
 CHUNKS = B // CHUNK
+QUADRANTS = 4
 WA_ROW = 4
-
-ITEMS = [(t, b0, 256, "g" if t == 1 else "h") for t in range(3) for b0 in (0, 256)]
+LAST = PACK - 1
+GPSIMD_D3_PLANE = 1
+ITEMS = [(t, b0) for t in range(LAST) for b0 in range(0, B, HALF)]
 
 
 def tile_list_group_spread_pl_kernel(tc, xt, fa, fb, wa_words, wa_scales, wb_words, wb_scales, offs, out_0, out_1, out_2):
@@ -34,7 +38,7 @@ def tile_list_group_spread_pl_kernel(tc, xt, fa, fb, wa_words, wa_scales, wb_wor
         ring = ctx.enter_context(tc.tile_pool(name="ring", bufs=2))
         psum = ctx.enter_context(tc.psum_pool(name="psum", bufs=1))
 
-        offsets = keep.tile([P, J // 16], U16, name="offsets")
+        offsets = keep.tile([P, J // STRIPE], U16, name="offsets")
         x_rows = xt.rearrange("(p t) c -> p t c", t=PACK)
         planes = [keep.tile([P, T], F32, name=f"plane{t}") for t in range(PACK)]
         wa_raw = keep.tile([P, N], I32, name="wa_raw")
@@ -44,30 +48,20 @@ def tile_list_group_spread_pl_kernel(tc, xt, fa, fb, wa_words, wa_scales, wb_wor
         fb_sb = keep.tile([P, PACK], F32, name="fb_sb")
         nc.vector.memset(ws_raw[:].bitcast(I32), 0)
 
-        def load_plane(t):
-            nc.sync.dma_start(out=planes[t][:], in_=x_rows[:, t, :])
-
-        def load_words(queue):
-            queue.dma_start(out=wb_raw[:].bitcast(I32), in_=wb_words[0].bitcast(I32))
-            queue.dma_start(out=wa_raw[:], in_=wa_words[0].rearrange("p n r -> p (n r)").bitcast(I32))
-
-        def load_scales(queue):
-            for q in range(4):
-                queue.dma_start(out=ws_raw[32 * q : 32 * q + 4, :].bitcast(I32), in_=wb_scales[0, 4 * q : 4 * q + 4, :].bitcast(I32))
-                queue.dma_start(out=ws_raw[32 * q + WA_ROW : 32 * q + WA_ROW + 4, :].bitcast(I32), in_=wa_scales[0, 4 * q : 4 * q + 4, :].bitcast(I32))
-
-        def load_factors(queue):
-            queue.dma_start(out=fb_sb[:], in_=fb.rearrange("(p t) o -> p (t o)", t=PACK))
-            queue.dma_start(out=fa_sb[:], in_=fa.rearrange("(p t) o -> p (t o)", t=PACK))
-
-        load_plane(0)
+        nc.sync.dma_start(out=planes[0][:], in_=x_rows[:, 0, :])
         nc.sync.dma_start(offsets[:], offs)
-        load_words(nc.sync)
-        load_factors(nc.scalar)
-        load_plane(1)
-        load_plane(2)
-        load_plane(3)
-        load_scales(nc.sync)
+        nc.sync.dma_start(out=wb_raw[:].bitcast(I32), in_=wb_words[0].bitcast(I32))
+        nc.sync.dma_start(out=wa_raw[:], in_=wa_words[0].rearrange("p n r -> p (n r)").bitcast(I32))
+        nc.scalar.dma_start(out=fb_sb[:], in_=fb.rearrange("(p t) o -> p (t o)", t=PACK))
+        nc.scalar.dma_start(out=fa_sb[:], in_=fa.rearrange("(p t) o -> p (t o)", t=PACK))
+        for t in range(1, PACK):
+            nc.sync.dma_start(out=planes[t][:], in_=x_rows[:, t, :])
+        for q in range(QUADRANTS):
+            rows = slice(4 * q, 4 * q + 4)
+            nc.sync.dma_start(out=ws_raw[32 * q : 32 * q + 4, :].bitcast(I32), in_=wb_scales[0, rows, :].bitcast(I32))
+            nc.sync.dma_start(
+                out=ws_raw[32 * q + WA_ROW : 32 * q + WA_ROW + 4, :].bitcast(I32), in_=wa_scales[0, rows, :].bitcast(I32)
+            )
 
         ident = keep.tile([P, P], F32, name="ident")
         make_identity(nc, ident[:])
@@ -82,97 +76,102 @@ def tile_list_group_spread_pl_kernel(tc, xt, fa, fb, wa_words, wa_scales, wb_wor
             for i, term in enumerate(terms):
                 nc.tensor.matmul(out, lhsT=term, rhs=ident[:], is_transpose=True, start=(i == 0), stop=(i == len(terms) - 1))
 
-        state = {}
+        def entries(b0):
+            return offsets[:, b0 * GROUP // STRIPE : (b0 + HALF) * GROUP // STRIPE]
 
-        def gather(t, b0, nb):
-            g = keep.tile([P, nb, 2, 2], F32, name=f"g{t}_{b0}")
-            cols = slice(b0 * GROUP // 16, (b0 + nb) * GROUP // 16)
-            nc.vector.tensor_copy(g[:].rearrange("p b h e -> p (b h e)"), planes[t][:].indirect(offsets[:, cols]))
+        def gather(t, b0):
+            g = keep.tile([P, HALF, 2, 2], F32, name=f"g{t}_{b0}")
+            nc.vector.tensor_copy(g[:].rearrange("p b h e -> p (b h e)"), planes[t][:].indirect(entries(b0)))
             return g
 
-        def differences(n):
-            t, b0, nb, eng = ITEMS[n]
-            g = gather(t, b0, nb)
-            neg = ring.tile([P, 2, nb], F32, name="neg", tag="neg", bufs=2)
-            nc.scalar.mul(neg[:].rearrange("p h b -> p b h"), g[:, :, :, 1], -1.0)
-            halves = ring.tile([P, nb, 2], F32, name="halves", tag="halves", bufs=3)
-            nc.gpsimd.tensor_tensor(halves[:], g[:, :, :, 0], g[:, :, :, 1], ALU.add)
-            d3 = ring.tile([P, nb], F32, name="d3", tag="d3", bufs=3)
-            if eng != "h":
-                nc.gpsimd.tensor_tensor(d3[:], halves[:, :, 0], halves[:, :, 1], ALU.subtract)
-            total = ring.tile([P, nb], F32, name="total", tag="total", bufs=3)
-            nc.gpsimd.tensor_tensor(total[:], halves[:, :, 0], halves[:, :, 1], ALU.add)
-            da = psum.tile([P, nb // CHUNK, 2, P], F32, name="da", tag="da", bufs=2)
-            for k in range(nb // CHUNK):
-                blk = slice(k * CHUNK, (k + 1) * CHUNK)
-                for h in range(2):
-                    add_transposed(da[:, k, h, :], [g[:, blk, h, 0], neg[:, h, blk]])
-            state[n] = (da, halves, d3, total)
+        def gather_pairs(t, b0):
+            g = keep.tile([P, 2, HALF, 2], F32, name=f"g{t}_{b0}")
+            nc.vector.tensor_copy(g[:].bitcast(U32).rearrange("p h b e -> p b h e"), planes[t][:].bitcast(U32).indirect(entries(b0)))
+            return g
 
-        def third(n):
-            t, b0, nb, eng = ITEMS[n]
-            da, halves, d3, total = state[n]
-            if eng == "h":
-                nc.scalar.mul(d3[:], halves[:, :, 1], -1.0)
-            db = psum.tile([P, nb // CHUNK, P], F32, name="db", tag="db", bufs=2)
-            for k in range(nb // CHUNK):
-                blk = slice(k * CHUNK, (k + 1) * CHUNK)
-                add_transposed(db[:, k, :], [halves[:, blk, 0], d3[:, blk]] if eng == "h" else [d3[:, blk]])
-            state[n] = (da, db, total)
+        blocks = [slice(k * CHUNK, (k + 1) * CHUNK) for k in range(HALF // CHUNK)]
+        held = {}
+
+        def pair_differences(n):
+            t, b0 = ITEMS[n]
+            g = gather_pairs(t, b0)
+            neg = ring.tile([P, 2, HALF], F32, name="neg", tag="neg", bufs=2)
+            nc.scalar.mul(neg[:], g[:, :, :, 1], -1.0)
+            halves = ring.tile([P, 2, HALF], F32, name="halves", tag="halves", bufs=3)
+            nc.gpsimd.tensor_tensor(halves[:], g[:, :, :, 0], g[:, :, :, 1], ALU.add)
+            d3_term = ring.tile([P, HALF], F32, name="d3", tag="d3", bufs=3)
+            if t == GPSIMD_D3_PLANE:
+                nc.gpsimd.tensor_tensor(d3_term[:], halves[:, 0, :], halves[:, 1, :], ALU.subtract)
+            total = ring.tile([P, HALF], F32, name="total", tag="total", bufs=3)
+            nc.gpsimd.tensor_tensor(total[:], halves[:, 0, :], halves[:, 1, :], ALU.add)
+            d12_t = psum.tile([P, len(blocks), 2, P], F32, name="da", tag="da", bufs=2)
+            for k, blk in enumerate(blocks):
+                for h in range(2):
+                    add_transposed(d12_t[:, k, h, :], [g[:, h, blk, 0], neg[:, h, blk]])
+            held[n] = (d12_t, halves, d3_term, total)
+
+        def third_difference(n):
+            t, b0 = ITEMS[n]
+            d12_t, halves, d3_term, total = held[n]
+            if t != GPSIMD_D3_PLANE:
+                nc.scalar.mul(d3_term[:], halves[:, 1, :], -1.0)
+            d3_t = psum.tile([P, len(blocks), P], F32, name="db", tag="db", bufs=2)
+            for k, blk in enumerate(blocks):
+                terms = [d3_term[:, blk]] if t == GPSIMD_D3_PLANE else [halves[:, 0, blk], d3_term[:, blk]]
+                add_transposed(d3_t[:, k, :], terms)
+            held[n] = (d12_t, d3_t, total)
 
         def squares(n):
-            t, b0, nb, eng = ITEMS[n]
-            da, db, total = state[n]
-            qa = ring.tile([P, nb // CHUNK, 2, P], F32, name="qa", tag="qa", bufs=2)
-            qb = ring.tile([P, nb // CHUNK, P], F32, name="qb", tag="qb", bufs=2)
-            nc.scalar.activation(qa[:], da[:], ACT.Square)
-            nc.scalar.activation(qb[:], db[:], ACT.Square, scale=0.5**0.5)
-            nc.scalar.activation(vu_planes[:, 0, t, b0 : b0 + nb], total[:], ACT.Copy, scale=fb4[:, t : t + 1])
-            spread = psum.tile([P, nb], F32, name="spread", tag="spread", bufs=2)
-            for k in range(nb // CHUNK):
-                add_transposed(spread[:, k * CHUNK : (k + 1) * CHUNK], [qa[:, k, 0, :], qa[:, k, 1, :], qb[:, k, :]])
-            state[n] = spread
+            t, b0 = ITEMS[n]
+            d12_t, d3_t, total = held[n]
+            q12_t = ring.tile([P, len(blocks), 2, P], F32, name="qa", tag="qa", bufs=2)
+            q3_t = ring.tile([P, len(blocks), P], F32, name="qb", tag="qb", bufs=2)
+            nc.scalar.activation(q12_t[:], d12_t[:], ACT.Square)
+            nc.scalar.activation(q3_t[:], d3_t[:], ACT.Square, scale=0.5**0.5)
+            nc.scalar.activation(vu_planes[:, 0, t, b0 : b0 + HALF], total[:], ACT.Copy, scale=fb4[:, t : t + 1])
+            spread = psum.tile([P, HALF], F32, name="spread", tag="spread", bufs=2)
+            for k, blk in enumerate(blocks):
+                add_transposed(spread[:, blk], [q12_t[:, k, 0, :], q12_t[:, k, 1, :], q3_t[:, k, :]])
+            held[n] = spread
 
-        def spread_out(n):
-            t, b0, nb, eng = ITEMS[n]
-            nc.scalar.activation(vu_planes[:, 1, t, b0 : b0 + nb], state[n][:], ACT.Copy, scale=fa8[:, t : t + 1])
+        def round_u(n):
+            t, b0 = ITEMS[n]
+            nc.scalar.activation(vu_planes[:, 1, t, b0 : b0 + HALF], held[n][:], ACT.Copy, scale=fa8[:, t : t + 1])
 
-        def last_plane(g, b0, nb):
-            t = PACK - 1
-            d12 = ring.tile([P, nb, 2], F32, name="d12", tag="d12")
+        def last_plane(g, b0):
+            fa8_last, fb4_last = fa8[:, LAST : LAST + 1], fb4[:, LAST : LAST + 1]
+            d12 = ring.tile([P, HALF, 2], F32, name="d12", tag="d12")
             nc.vector.tensor_tensor(d12[:], g[:, :, :, 0], g[:, :, :, 1], ALU.subtract)
-            s12 = ring.tile([P, nb, 2], F32, name="s12", tag="s12")
+            s12 = ring.tile([P, HALF, 2], F32, name="s12", tag="s12")
             nc.vector.tensor_tensor(s12[:], g[:, :, :, 0], g[:, :, :, 1], ALU.add)
-            q12 = ring.tile([P, nb, 2], F32, name="q12", tag="q12")
+            q12 = ring.tile([P, HALF, 2], F32, name="q12", tag="q12")
             nc.scalar.activation(q12[:], d12[:], ACT.Square)
-            e3 = ring.tile([P, nb], F32, name="e3", tag="e3")
-            nc.vector.tensor_tensor(e3[:], s12[:, :, 0], s12[:, :, 1], ALU.subtract)
-            s4 = ring.tile([P, nb], F32, name="s4", tag="s4")
+            d3 = ring.tile([P, HALF], F32, name="e3", tag="e3")
+            nc.vector.tensor_tensor(d3[:], s12[:, :, 0], s12[:, :, 1], ALU.subtract)
+            s4 = ring.tile([P, HALF], F32, name="s4", tag="s4")
             nc.vector.tensor_tensor(s4[:], s12[:, :, 0], s12[:, :, 1], ALU.add)
-            q3 = ring.tile([P, nb], F32, name="q3", tag="q3")
-            nc.scalar.activation(q3[:], e3[:], ACT.Square, scale=0.5**0.5)
-            q3f = ring.tile([P, nb], F32, name="q3f", tag="q3f")
-            nc.scalar.activation(q3f[:], q3[:], ACT.Copy, scale=fa8[:, t : t + 1])
-            nc.scalar.activation(vu_planes[:, 0, t, b0 : b0 + nb], s4[:], ACT.Copy, scale=fb4[:, t : t + 1])
-            q = ring.tile([P, nb], F32, name="q", tag="q")
-            nc.vector.tensor_tensor(q[:], q12[:, :, 0], q12[:, :, 1], ALU.add)
-            nc.vector.scalar_tensor_tensor(vu_planes[:, 1, t, b0 : b0 + nb], q[:], fa8[:, t : t + 1], q3f[:], ALU.mult, ALU.add)
+            q3 = ring.tile([P, HALF], F32, name="q3", tag="q3")
+            nc.scalar.activation(q3[:], d3[:], ACT.Square, scale=0.5**0.5)
+            q3f = ring.tile([P, HALF], F32, name="q3f", tag="q3f")
+            nc.scalar.activation(q3f[:], q3[:], ACT.Copy, scale=fa8_last)
+            nc.scalar.activation(vu_planes[:, 0, LAST, b0 : b0 + HALF], s4[:], ACT.Copy, scale=fb4_last)
+            q12_sum = ring.tile([P, HALF], F32, name="q", tag="q")
+            nc.vector.tensor_tensor(q12_sum[:], q12[:, :, 0], q12[:, :, 1], ALU.add)
+            nc.vector.scalar_tensor_tensor(
+                vu_planes[:, 1, LAST, b0 : b0 + HALF], q12_sum[:], fa8_last, q3f[:], ALU.mult, ALU.add
+            )
 
         wa = keep.tile([P, PACK, P], I32, name="wa", align_bytes=64)
         wb = keep.tile([P, PACK, P, 2], U8, name="wb", align_bytes=64)
         ws = keep.tile([P, PACK, P], U8, name="ws", align_bytes=64)
 
-        def deal_weights():
-            nc.gpsimd.tensor_copy(wb[:], wb_raw[:].rearrange("p (m t e) -> p t m e", t=PACK, e=2))
-            nc.gpsimd.tensor_copy(wa[:], wa_raw[:].rearrange("p (m t) -> p t m", t=PACK))
-            nc.gpsimd.tensor_copy(ws[:], ws_raw[:].rearrange("p (m t) -> p t m", t=PACK))
-
         y_codes = keep.tile([P, B], U32, name="y_codes", align_bytes=64)
         y_scales = keep.tile([P, B], U8, name="y_scales", align_bytes=64)
         out_rows = out_0.rearrange("(p t) b -> p t b", t=PACK)
         out_words = out_1[0].rearrange("p b r -> p (b r)").bitcast(I32)
+        operands = {}
 
-        def operands(c):
+        def quantise_operands(c):
             cols = slice(c * CHUNK, (c + 1) * CHUNK)
             vu = ring.tile([P, 2, CHUNK, PACK], BF16, name="vu", tag="vu", bufs=CHUNKS, align_bytes=64)
             for i in range(2):
@@ -182,12 +181,14 @@ def tile_list_group_spread_pl_kernel(tc, xt, fa, fb, wa_words, wa_scales, wb_wor
             codes = ring.tile([P, 2, CHUNK], U32, name="codes", tag="codes", bufs=CHUNKS, align_bytes=64)
             scales = ring.tile([P, 2, CHUNK], U8, name="scales", tag="scales", bufs=CHUNKS, align_bytes=64)
             for i in range(2):
-                nc.vector.quantize_mx(out=codes[:, i, :].bitcast(E4M3), scales=scales[:, i, :], in_=vu[:, i].rearrange("p b t -> p (b t)"))
-            state["q", c] = (codes, scales)
+                nc.vector.quantize_mx(
+                    out=codes[:, i, :].bitcast(E4M3), scales=scales[:, i, :], in_=vu[:, i].rearrange("p b t -> p (b t)")
+                )
+            operands[c] = (codes, scales)
 
         def product(c):
             cols = slice(c * CHUNK, (c + 1) * CHUNK)
-            codes, scales = state["q", c]
+            codes, scales = operands[c]
             y = psum.tile([P, PACK, CHUNK], F32, name="y", tag="y", bufs=2)
             for t in range(PACK):
                 nc.tensor.matmul_mx(
@@ -209,24 +210,27 @@ def tile_list_group_spread_pl_kernel(tc, xt, fa, fb, wa_words, wa_scales, wb_wor
             )
             nc.sync.dma_start(out=out_words[:, cols], in_=y_codes[:, cols].bitcast(I32))
 
-        deal_weights()
-        last = len(ITEMS)
-        for n in range(last + 2):
-            if n < last:
-                differences(n)
-            if 2 <= n:
-                spread_out(n - 2)
-            if 1 <= n <= last:
+        nc.gpsimd.tensor_copy(wb[:], wb_raw[:].rearrange("p (m t e) -> p t m e", t=PACK, e=2))
+        nc.gpsimd.tensor_copy(wa[:], wa_raw[:].rearrange("p (m t) -> p t m", t=PACK))
+        nc.gpsimd.tensor_copy(ws[:], ws_raw[:].rearrange("p (m t) -> p t m", t=PACK))
+
+        for n in range(len(ITEMS) + 2):
+            if n < len(ITEMS):
+                pair_differences(n)
+            if n >= 2:
+                round_u(n - 2)
+            if 1 <= n <= len(ITEMS):
                 squares(n - 1)
-            if n < last:
-                third(n)
-        tail = [(gather(PACK - 1, b0, 256), b0) for b0 in range(0, B, 256)]
-        for g, b0 in tail:
-            last_plane(g, b0, 256)
-            for c in range(b0 // CHUNK, (b0 + 256) // CHUNK):
-                operands(c)
-            for c in range(b0 // CHUNK, (b0 + 256) // CHUNK):
+            if n < len(ITEMS):
+                third_difference(n)
+        last_gathers = [(gather(LAST, b0), b0) for b0 in range(0, B, HALF)]
+        for g, b0 in last_gathers:
+            last_plane(g, b0)
+            chunks = range(b0 // CHUNK, (b0 + HALF) // CHUNK)
+            for c in chunks:
+                quantise_operands(c)
+            for c in chunks:
                 product(c)
-        for q in range(4):
+        for q in range(QUADRANTS):
             queue = nc.sync if q % 2 == 0 else nc.scalar
             queue.dma_start(out=out_2[0, 4 * q : 4 * q + 4, :].bitcast(I32), in_=y_scales[32 * q : 32 * q + 4, :].bitcast(I32))

from contextlib import ExitStack

import concourse.mybir as mybir
from concourse.masks import make_identity

K, T, J, B, N = 512, 2048, 2048, 512, 512
FLOPS = 2 * 2 * K * N * B

F32 = mybir.dt.float32
BF16 = mybir.dt.bfloat16
I32 = mybir.dt.int32
U32 = mybir.dt.uint32
U16 = mybir.dt.uint16
U8 = mybir.dt.uint8
E4M3 = mybir.dt.float8_e4m3fn_x4
E2M1 = mybir.dt.float4_e2m1fn_x4
ACT = mybir.ActivationFunctionType
ALU = mybir.AluOpType

P = 128
PACK = 4
GROUP = J // B
STRIPE = 16
HALF = B // 2
CHUNK = 128
CHUNKS = B // CHUNK
QUADRANTS = 4
WA_ROW = 4
LAST = PACK - 1
GPSIMD_D3_PLANE = 1
ITEMS = [(t, b0) for t in range(LAST) for b0 in range(0, B, HALF)]


def tile_list_group_spread_pl_kernel(tc, xt, fa, fb, wa_words, wa_scales, wb_words, wb_scales, offs, out_0, out_1, out_2):
    nc = tc.nc
    with ExitStack() as ctx:
        keep = ctx.enter_context(tc.tile_pool(name="keep", bufs=1))
        ring = ctx.enter_context(tc.tile_pool(name="ring", bufs=2))
        psum = ctx.enter_context(tc.psum_pool(name="psum", bufs=1))

        offsets = keep.tile([P, J // STRIPE], U16, name="offsets")
        x_rows = xt.rearrange("(p t) c -> p t c", t=PACK)
        planes = [keep.tile([P, T], F32, name=f"plane{t}") for t in range(PACK)]
        wa_raw = keep.tile([P, N], I32, name="wa_raw")
        wb_raw = keep.tile([P, 2 * N], U8, name="wb_raw")
        ws_raw = keep.tile([P, N], U8, name="ws_raw")
        fa_sb = keep.tile([P, PACK], F32, name="fa_sb")
        fb_sb = keep.tile([P, PACK], F32, name="fb_sb")
        nc.vector.memset(ws_raw[:].bitcast(I32), 0)

        nc.sync.dma_start(out=planes[0][:], in_=x_rows[:, 0, :])
        nc.sync.dma_start(offsets[:], offs)
        nc.sync.dma_start(out=wb_raw[:].bitcast(I32), in_=wb_words[0].bitcast(I32))
        nc.sync.dma_start(out=wa_raw[:], in_=wa_words[0].rearrange("p n r -> p (n r)").bitcast(I32))
        nc.scalar.dma_start(out=fb_sb[:], in_=fb.rearrange("(p t) o -> p (t o)", t=PACK))
        nc.scalar.dma_start(out=fa_sb[:], in_=fa.rearrange("(p t) o -> p (t o)", t=PACK))
        for t in range(1, PACK):
            nc.sync.dma_start(out=planes[t][:], in_=x_rows[:, t, :])
        for q in range(QUADRANTS):
            rows = slice(4 * q, 4 * q + 4)
            nc.sync.dma_start(out=ws_raw[32 * q : 32 * q + 4, :].bitcast(I32), in_=wb_scales[0, rows, :].bitcast(I32))
            nc.sync.dma_start(
                out=ws_raw[32 * q + WA_ROW : 32 * q + WA_ROW + 4, :].bitcast(I32), in_=wa_scales[0, rows, :].bitcast(I32)
            )

        ident = keep.tile([P, P], F32, name="ident")
        make_identity(nc, ident[:])
        fa8 = keep.tile([P, PACK], F32, name="fa8")
        fb4 = keep.tile([P, PACK], F32, name="fb4")
        nc.scalar.mul(fa8[:], fa_sb[:], 0.125)
        nc.scalar.mul(fb4[:], fb_sb[:], 0.25)

        vu_planes = keep.tile([P, 2, PACK, B], BF16, name="vu_planes")

        def add_transposed(out, terms):
            for i, term in enumerate(terms):
                nc.tensor.matmul(out, lhsT=term, rhs=ident[:], is_transpose=True, start=(i == 0), stop=(i == len(terms) - 1))

        def entries(b0):
            return offsets[:, b0 * GROUP // STRIPE : (b0 + HALF) * GROUP // STRIPE]

        def gather(t, b0):
            g = keep.tile([P, HALF, 2, 2], F32, name=f"g{t}_{b0}")
            nc.vector.tensor_copy(g[:].rearrange("p b h e -> p (b h e)"), planes[t][:].indirect(entries(b0)))
            return g

        def gather_pairs(t, b0):
            g = keep.tile([P, 2, HALF, 2], F32, name=f"g{t}_{b0}")
            nc.vector.tensor_copy(g[:].bitcast(U32).rearrange("p h b e -> p b h e"), planes[t][:].bitcast(U32).indirect(entries(b0)))
            return g

        blocks = [slice(k * CHUNK, (k + 1) * CHUNK) for k in range(HALF // CHUNK)]
        held = {}

        def pair_differences(n):
            t, b0 = ITEMS[n]
            g = gather_pairs(t, b0)
            neg = ring.tile([P, 2, HALF], F32, name="neg", tag="neg", bufs=2)
            nc.scalar.mul(neg[:], g[:, :, :, 1], -1.0)
            halves = ring.tile([P, 2, HALF], F32, name="halves", tag="halves", bufs=3)
            nc.gpsimd.tensor_tensor(halves[:], g[:, :, :, 0], g[:, :, :, 1], ALU.add)
            d3_term = ring.tile([P, HALF], F32, name="d3", tag="d3", bufs=3)
            if t == GPSIMD_D3_PLANE:
                nc.gpsimd.tensor_tensor(d3_term[:], halves[:, 0, :], halves[:, 1, :], ALU.subtract)
            total = ring.tile([P, HALF], F32, name="total", tag="total", bufs=3)
            nc.gpsimd.tensor_tensor(total[:], halves[:, 0, :], halves[:, 1, :], ALU.add)
            d12_t = psum.tile([P, len(blocks), 2, P], F32, name="da", tag="da", bufs=2)
            for k, blk in enumerate(blocks):
                for h in range(2):
                    add_transposed(d12_t[:, k, h, :], [g[:, h, blk, 0], neg[:, h, blk]])
            held[n] = (d12_t, halves, d3_term, total)

        def third_difference(n):
            t, b0 = ITEMS[n]
            d12_t, halves, d3_term, total = held[n]
            if t != GPSIMD_D3_PLANE:
                nc.scalar.mul(d3_term[:], halves[:, 1, :], -1.0)
            d3_t = psum.tile([P, len(blocks), P], F32, name="db", tag="db", bufs=2)
            for k, blk in enumerate(blocks):
                terms = [d3_term[:, blk]] if t == GPSIMD_D3_PLANE else [halves[:, 0, blk], d3_term[:, blk]]
                add_transposed(d3_t[:, k, :], terms)
            held[n] = (d12_t, d3_t, total)

        def squares(n):
            t, b0 = ITEMS[n]
            d12_t, d3_t, total = held[n]
            q12_t = ring.tile([P, len(blocks), 2, P], F32, name="qa", tag="qa", bufs=2)
            q3_t = ring.tile([P, len(blocks), P], F32, name="qb", tag="qb", bufs=2)
            nc.scalar.activation(q12_t[:], d12_t[:], ACT.Square)
            nc.scalar.activation(q3_t[:], d3_t[:], ACT.Square, scale=0.5**0.5)
            nc.scalar.activation(vu_planes[:, 0, t, b0 : b0 + HALF], total[:], ACT.Copy, scale=fb4[:, t : t + 1])
            spread = psum.tile([P, HALF], F32, name="spread", tag="spread", bufs=2)
            for k, blk in enumerate(blocks):
                add_transposed(spread[:, blk], [q12_t[:, k, 0, :], q12_t[:, k, 1, :], q3_t[:, k, :]])
            held[n] = spread

        def round_u(n):
            t, b0 = ITEMS[n]
            nc.scalar.activation(vu_planes[:, 1, t, b0 : b0 + HALF], held[n][:], ACT.Copy, scale=fa8[:, t : t + 1])

        def last_plane(g, b0):
            fa8_last, fb4_last = fa8[:, LAST : LAST + 1], fb4[:, LAST : LAST + 1]
            d12 = ring.tile([P, HALF, 2], F32, name="d12", tag="d12")
            nc.vector.tensor_tensor(d12[:], g[:, :, :, 0], g[:, :, :, 1], ALU.subtract)
            s12 = ring.tile([P, HALF, 2], F32, name="s12", tag="s12")
            nc.vector.tensor_tensor(s12[:], g[:, :, :, 0], g[:, :, :, 1], ALU.add)
            q12 = ring.tile([P, HALF, 2], F32, name="q12", tag="q12")
            nc.scalar.activation(q12[:], d12[:], ACT.Square)
            d3 = ring.tile([P, HALF], F32, name="e3", tag="e3")
            nc.vector.tensor_tensor(d3[:], s12[:, :, 0], s12[:, :, 1], ALU.subtract)
            s4 = ring.tile([P, HALF], F32, name="s4", tag="s4")
            nc.vector.tensor_tensor(s4[:], s12[:, :, 0], s12[:, :, 1], ALU.add)
            q3 = ring.tile([P, HALF], F32, name="q3", tag="q3")
            nc.scalar.activation(q3[:], d3[:], ACT.Square, scale=0.5**0.5)
            q3f = ring.tile([P, HALF], F32, name="q3f", tag="q3f")
            nc.scalar.activation(q3f[:], q3[:], ACT.Copy, scale=fa8_last)
            nc.scalar.activation(vu_planes[:, 0, LAST, b0 : b0 + HALF], s4[:], ACT.Copy, scale=fb4_last)
            q12_sum = ring.tile([P, HALF], F32, name="q", tag="q")
            nc.vector.tensor_tensor(q12_sum[:], q12[:, :, 0], q12[:, :, 1], ALU.add)
            nc.vector.scalar_tensor_tensor(
                vu_planes[:, 1, LAST, b0 : b0 + HALF], q12_sum[:], fa8_last, q3f[:], ALU.mult, ALU.add
            )

        wa = keep.tile([P, PACK, P], I32, name="wa", align_bytes=64)
        wb = keep.tile([P, PACK, P, 2], U8, name="wb", align_bytes=64)
        ws = keep.tile([P, PACK, P], U8, name="ws", align_bytes=64)

        y_codes = keep.tile([P, B], U32, name="y_codes", align_bytes=64)
        y_scales = keep.tile([P, B], U8, name="y_scales", align_bytes=64)
        out_rows = out_0.rearrange("(p t) b -> p t b", t=PACK)
        out_words = out_1[0].rearrange("p b r -> p (b r)").bitcast(I32)
        operands = {}

        def quantise_operands(c):
            cols = slice(c * CHUNK, (c + 1) * CHUNK)
            vu = ring.tile([P, 2, CHUNK, PACK], BF16, name="vu", tag="vu", bufs=CHUNKS, align_bytes=64)
            for i in range(2):
                nc.vector.tensor_copy(
                    vu[:, i].rearrange("p (c j) t -> p c t j", j=4), vu_planes[:, i, :, cols].rearrange("p t (c j) -> p c t j", j=4)
                )
            codes = ring.tile([P, 2, CHUNK], U32, name="codes", tag="codes", bufs=CHUNKS, align_bytes=64)
            scales = ring.tile([P, 2, CHUNK], U8, name="scales", tag="scales", bufs=CHUNKS, align_bytes=64)
            for i in range(2):
                nc.vector.quantize_mx(
                    out=codes[:, i, :].bitcast(E4M3), scales=scales[:, i, :], in_=vu[:, i].rearrange("p b t -> p (b t)")
                )
            operands[c] = (codes, scales)

        def product(c):
            cols = slice(c * CHUNK, (c + 1) * CHUNK)
            codes, scales = operands[c]
            y = psum.tile([P, PACK, CHUNK], F32, name="y", tag="y", bufs=2)
            for t in range(PACK):
                nc.tensor.matmul_mx(
                    out=y[:, t, :], lhsT=wb[:, t, :, :].rearrange("p m e -> p (m e)").bitcast(E2M1), lhsT_scale=ws[:, t, :],
                    rhs=codes[:, 0, :].bitcast(E4M3), rhs_scale=scales[:, 0, :], start=(t == 0), stop=False,
                )
            for t in range(PACK):
                nc.tensor.matmul_mx(
                    out=y[:, t, :], lhsT=wa[:, t, :].bitcast(E4M3), lhsT_scale=ws[WA_ROW:P, t, :],
                    rhs=codes[:, 1, :].bitcast(E4M3), rhs_scale=scales[:, 1, :], start=False, stop=(t == PACK - 1),
                )
            y16 = ring.tile([P, CHUNK, PACK], BF16, name="y16", tag="y16", bufs=CHUNKS, align_bytes=64)
            y32 = ring.tile([P, PACK, CHUNK], F32, name="y32", tag="y32", bufs=CHUNKS)
            nc.scalar.copy(y16[:], y[:].rearrange("p t b -> p b t"))
            nc.scalar.copy(y32[:], y[:])
            nc.sync.dma_start(out=out_rows[:, :, cols], in_=y32[:])
            nc.vector.quantize_mx(
                out=y_codes[:, cols].bitcast(E4M3), scales=y_scales[:, cols], in_=y16[:].rearrange("p b t -> p (b t)")
            )
            nc.sync.dma_start(out=out_words[:, cols], in_=y_codes[:, cols].bitcast(I32))

        nc.gpsimd.tensor_copy(wb[:], wb_raw[:].rearrange("p (m t e) -> p t m e", t=PACK, e=2))
        nc.gpsimd.tensor_copy(wa[:], wa_raw[:].rearrange("p (m t) -> p t m", t=PACK))
        nc.gpsimd.tensor_copy(ws[:], ws_raw[:].rearrange("p (m t) -> p t m", t=PACK))

        for n in range(len(ITEMS) + 2):
            if n < len(ITEMS):
                pair_differences(n)
            if n >= 2:
                round_u(n - 2)
            if 1 <= n <= len(ITEMS):
                squares(n - 1)
            if n < len(ITEMS):
                third_difference(n)
        last_gathers = [(gather(LAST, b0), b0) for b0 in range(0, B, HALF)]
        for g, b0 in last_gathers:
            last_plane(g, b0)
            chunks = range(b0 // CHUNK, (b0 + HALF) // CHUNK)
            for c in chunks:
                quantise_operands(c)
            for c in chunks:
                product(c)
        for q in range(QUADRANTS):
            queue = nc.sync if q % 2 == 0 else nc.scalar
            queue.dma_start(out=out_2[0, 4 * q : 4 * q + 4, :].bitcast(I32), in_=y_scales[32 * q : 32 * q + 4, :].bitcast(I32))
